import numpy as np, ml_dtypes
CORES = [24,25,26,27,28,29,30,31]
N = 8
BF = ml_dtypes.bfloat16
def gentries(a):
    return np.ascontiguousarray(a.reshape(8, 16, -1).transpose(0, 2, 1)).reshape(8, -1)
def gtable(e):
    e = np.asarray(e); return np.ascontiguousarray(e.reshape(8, -1, 16).transpose(0, 2, 1)).reshape(128, -1).astype(np.int32)
V, L, D, T, RO = 2048, 256, 16, 1, 8
def rows_of(rng, a, b):
    u = np.concatenate([a, b]); w = np.concatenate([b, a])
    return w[np.argsort(u + 0.5 * rng.random(u.size))].reshape(V, D)
def graph(rng, kind):
    i = np.arange(V)
    if kind == 2:
        m = i.reshape(-1, 2, D); a = np.repeat(m[:, 0], D, axis=1).reshape(-1); b = np.tile(m[:, 1], (1, D)).reshape(-1)
    elif kind == 1:
        s = 1 + rng.permutation(V - 1)[:D]; w = i[:, None] ^ s; keep = w > i[:, None]
        a = np.repeat(i[:, None], D, axis=1)[keep]; b = w[keep]
    else:
        s = 1 + rng.permutation(V // 2 - 1)[:D // 2]; a = np.repeat(i, D // 2); b = ((i[:, None] + s) & (V - 1)).reshape(-1)
        turn = rng.random(a.size) < 0.5; a, b = np.where(turn, b, a), np.where(turn, a, b)
        o = rng.permutation(a.size); k = a.size // 2; p, q = o[:k], o[k:2 * k]
        def key(u, w): return np.minimum(u, w) * V + np.maximum(u, w)
        new = np.concatenate([key(a[p], b[q]), key(a[q], b[p])])
        z, inv, cnt = np.unique(new, return_inverse=True, return_counts=True)
        no = np.isin(new, key(a, b)) | (cnt[inv.reshape(-1)] > 1); no = no[:k] | no[k:] | (a[p] == b[q]) | (a[q] == b[p])
        p, q = p[~no], q[~no]; bp, bq = b[p].copy(), b[q].copy(); b[p] = bq; b[q] = bp
    m = rng.permutation(V)
    return rows_of(rng, m[a], m[b])
def graphs(rng, kinds):
    return np.stack([np.stack([graph(rng, int(kinds[r, g])) for g in range(8)]) for r in range(N)])
def parts(rng):
    return (rng.integers(-15, 16, (N, 8, 16, V)), rng.integers(-15, 16, (N, 8, 16, L)), rng.integers(-15, 16, (N, 8, 16, L)), rng.integers(-255, 256, (N, 8, 16, 1)),
            rng.integers(0, V, (N, 8, L)), rng.integers(0, D + T, (N, 8, L)))
def pack(nbs, x, c, y, h, v, j):
    def bf(a): return np.ascontiguousarray(a.reshape(N, 128, -1)).astype(np.float32).astype(BF)
    return {"adj": np.ascontiguousarray(nbs.transpose(0, 1, 3, 2).reshape(N, 8 * D, V)).astype(np.int32), "x": bf(x), "c0": bf(c), "y0": bf(y), "h": bf(h),
            "v0": np.stack([gtable(a) for a in v]), "j0": np.stack([gtable(a) for a in j])}
def setup_inputs(rng):
    return pack(graphs(rng, rng.choice(np.array([0, 0, 0, 1]), (N, 8))), *parts(rng))
def setup_inputs_ties(rng):
    x, c, y, h, v, j = parts(rng); pool = rng.integers(-1, 2, (N, 8, 16, 6))
    x = np.take_along_axis(pool, np.broadcast_to(rng.integers(0, 6, (N, 8, 1, V)), (N, 8, 16, V)), 3)
    c = rng.integers(-1, 2, c.shape) * (rng.random((N, 8, 1, L)) < 0.9)
    y = rng.integers(-1, 2, y.shape)
    return pack(graphs(rng, rng.choice(np.array([0, 1, 2]), (N, 8))), x, c, y, h, v, j)
def setup_inputs_tops(rng):
    x, c, y, h, v, j = parts(rng); k = L // 2
    c[..., :k] = 0; j[..., :k] = rng.integers(D, D + T, (N, 8, k))
    h[:, :4, 0] = -1; h[:, 0, 1:6] = 128; h[:, 1, 1:6] = -128; h[:, 4:6] = 255; h[:, 6:] = -255
    y[..., 0:3] = 0; y[:, :, 0, 1] = 1; y[:, :, 0, 2] = 2; y[..., 3] = 15; y[..., 4] = -15
    y[..., 5:k:2] = np.abs(y[..., 5:k:2])
    for i in range(4):
        y[:, :2, :, 5 + i] = 0
        y[:, :2, 1:6, 5 + i] = (1, -1, 1, -1)[i] * np.clip((1, 1, 2, 2)[i] * V // 128 - 15 * np.arange(5), 0, 15)
    v[..., 9:13] = (np.add.reduce(h * y, axis=2) & (V - 1))[..., 9:13]
    nbs = graphs(rng, rng.choice(np.array([0, 1]), (N, 8)))
    for r in range(N):
        for g in range(8):
            n = int(rng.integers(0, V)); q = int(rng.integers(0, D)); w = int(nbs[r, g, n, q])
            x[r, g, :, n] = 15; x[r, g, :, w] = -15
            v[r, g, k:k + 4] = n; j[r, g, k:k + 4] = np.array([q, q, D, D]); c[r, g, :, k:k + 4] = np.array([15, -15, 15, -15])
            m = int(rng.choice(np.setdiff1d(np.arange(V), np.concatenate([np.array([n, w]), nbs[r, g, n], nbs[r, g, w]]))))
            t = rng.integers(2, 6, D); t[0] = 5; t[1] = 6; t[D - 1] = 1
            x[r, g][:, nbs[r, g, m]] = 15 - (np.argsort(rng.random((16, D)), axis=0) < t)
            p, z = ((3, 1), (10, 2))[g % 2]; x[r, g, :, m] = 15 - z * (rng.permutation(16) < p)
            v[r, g, k + 4:k + 8] = m; j[r, g, k + 4:k + 8] = np.array([D, D, 0, 0]); c[r, g, :, k + 4:k + 8] = np.array([15, -15, 15, -15])
    return pack(nbs, x, c, y, h, v, j)
def setup_inputs_deep(rng):
    x, c, y, h, v, j = parts(rng); i = np.arange(V); q = i * 3390 // V
    col = np.concatenate([(q[None, :] // 15 + np.arange(15)[:, None]) // 15, (q % 15)[None, :]])
    w = (i[:, None] + np.concatenate([np.arange(-(D // 2), 0), np.arange(1, D // 2 + 1)])) & (V - 1)
    nbs = np.zeros((N, 8, V, D), np.int64); way = np.array([15] * 15 + [1])
    for r in range(N):
        for g in range(8):
            m = rng.permutation(V); u = (w, w[:, ::-1], rng.permuted(w, axis=1), rng.permuted(w, axis=1))[g % 4]
            nbs[r, g, m] = m[u]; x[r, g][:, m] = col
            c[r, g] = way[:, None] * np.where(rng.random(L) < 0.7, 1, -1)
    return pack(nbs, x, c, y, h, v, j)
def setup_inputs_alike(rng):
    x, c, y, h, v, j = parts(rng)
    v[:, 0::4] = rng.integers(0, V, (N, 2, 1)); v[:, 1::4] = rng.choice(np.array([0, V - 1]), (N, 2, L))
    j[:, 0::4] = np.arange(L) % (D + T); c[:, 2] = c[:, 2, :, :1]
    j[:, 3::3] = rng.integers(D, D + T, (N, 2, L)); c[:, 6] = 0; j[:, 5] = 0
    for r in range(N):
        n = int(rng.integers(0, V)); x[r, 7, :, n] = 15; v[r, 7] = n
    c[:, 7] = 15; j[:, 7] = rng.integers(0, D, (N, L))
    kinds = np.tile(np.array([2, 0, 2, 1, 0, 2, 1, 2]), (N, 1))
    return pack(graphs(rng, kinds), x, c, y, h, v, j)
def setup_inputs_spread(rng):
    x, c, y, h, v, j = parts(rng)
    def size(a, top): return np.sign(a) * ((np.abs(a) * np.exp2(-top * rng.random(a.shape[:2] + (1, a.shape[3])))).astype(np.int64))
    x = size(x, 5) * (rng.random((N, 8, 1, V)) > 0.0625); c = size(c, 4); y = size(y, 4); h = size(h, 7)
    v = (V * rng.random((N, 8, L)) ** 4).astype(np.int64)
    return pack(graphs(rng, rng.choice(np.array([0, 0, 1]), (N, 8))), x, c, y, h, np.minimum(v, V - 1), j)
def check_inputs(d):
    bad = []
    for k, lo, hi in (("adj", 0, V - 1), ("x", -15, 15), ("c0", -15, 15), ("y0", -15, 15), ("h", -255, 255), ("v0", 0, V - 1), ("j0", 0, D + T - 1)):
        a = np.asarray(d[k]).astype(np.float32)
        if not (np.min(a) >= lo and np.max(a) <= hi and np.all(a == np.floor(a))): bad.append("range of " + k)
    me = np.arange(V)[:, None]; own = twice = oneway = False
    for a in np.asarray(d["adj"]).astype(np.int64).reshape(N * 8, D, V):
        w = np.ascontiguousarray(a.T); s = np.sort(w, axis=1)
        own = own or bool(np.any(w == me)); twice = twice or bool(np.any(s[:, 1:] == s[:, :-1]))
        oneway = oneway or bool(np.any(np.sort((me * V + w).reshape(-1)) != np.sort((w * V + me).reshape(-1))))
    if own: bad.append("adj: a node is its own neighbour")
    if twice: bad.append("adj: a neighbour stands twice at one node")
    if oneway: bad.append("adj: an edge goes one way only")
    return bad
def reference(adj, x, c0, y0, h, v0, j0):
    P = N * 8
    nbs = np.ascontiguousarray(adj.reshape(P, D, V).transpose(0, 2, 1)).astype(np.int64)
    def turned(a): return np.ascontiguousarray(a.astype(np.float32).reshape(P, 16, -1).transpose(0, 2, 1)).astype(np.int32)
    xs, c, y, hs = turned(x), turned(c0), turned(y0), turned(h)
    v = np.stack([gentries(a) for a in v0]).reshape(P, L).astype(np.int64); j = np.stack([gentries(a) for a in j0]).reshape(P, L).astype(np.int64)
    b = np.arange(P)[:, None]; b3 = b[:, :, None]
    def parent(e, c):
        near = nbs[b, e]
        s = np.einsum("pldi,pli->pld", xs[b3, near], c); mine = np.einsum("pli,pli->pl", xs[b, e], c)
        best = np.argmax(s, axis=2)[:, :, None]
        return np.where(np.take_along_axis(s, best, 2)[:, :, 0] > mine, np.take_along_axis(near, best, 2)[:, :, 0], e)
    for step in range(1, RO + 1):
        back = j >= D; nv = v; nj = j + T; found = np.zeros((P, L), bool); fv = v
        for t in range(T):
            ok = ~back & (j + t < D)
            w = np.where(ok, nbs[b, v, np.minimum(j + t, D - 1)], v)
            f = parent(w, c)
            if t == 0: fv = f
            hit = ok & ~found & (f == v)
            nv = np.where(hit, w, nv); nj = np.where(hit, 0, nj); found = found | hit
        at = np.argmax(nbs[b, fv] == v[:, :, None], axis=2)
        again = np.add.reduce(hs.astype(np.int64) * y, axis=2) & (V - 1)
        up = back & (fv != v); top = back & (fv == v)
        v = np.where(up, fv, np.where(top, again, nv)); j = np.where(up, 1 + at, np.where(top, 0, nj))
        if step % 2 == 0:
            xv = xs[b, v]
            y = np.roll(xv.reshape(N, 8, L, 16), 1, axis=0).reshape(P, L, 16)
            c = np.clip(c + np.sign(y - xv), -15, 15)
    return {"vo": v.reshape(N, 8, L).astype(np.float32), "jo": j.reshape(N, 8, L).astype(np.float32),
            "co": np.ascontiguousarray(c.transpose(0, 2, 1)).reshape(N, 128, L).astype(np.float32)}

@@ -1,0 +1,420 @@
+from concourse.mybir import AluOpType as A, ActivationFunctionType as F
+
+LS = [128, 128]
+PIECE = 16
+NV = 2
+H = "float16"
+NENG = 8
+MODELS = [(1.56, 100.0, 0.5, 0.0), (1.2, 150.0, 0.5, 20.0), (1.9, 60.0, 0.6, 0.0)]
+ITER = 900
+STEPS = 8
+NS = len(LS)
+L0 = [sum(LS[:i]) for i in range(NS)]
+SC = float(2 ** 17)
+f32, bf, i32, u16_ = "float32", "bfloat16", "int32", "uint16"
+
+SCRATCH = {k: ("sbuf", [128] + sh, d) for k, sh, d in (
+    ("adjs", [2048], i32), ("adjp", [2048], i32), ("adjd", [2048], i32), ("idt", [2048], f32), ("xs", [2048], bf),
+    ("i512", [512], f32), ("i16", [16], i32), ("v0s", [16], i32), ("j0s", [16], i32), ("j16", [16], u16_),
+    ("v0h", [16], H), ("b0h", [16], H), ("bv0", [16], H), ("cs", [256], bf), ("y0s", [256], bf), ("hs", [8], bf),
+    ("cof", [256], f32), ("vr", [256], f32), ("jr", [256], f32), ("ia", [128], f32), ("ib", [128], f32), ("ic", [128], f32),
+    ("idn", [128], f32), ("ie", [144], i32), ("im", [8], i32), ("im2", [8], i32), ("imf", [8], f32), ("io1", [16], i32),
+    ("io2", [16], i32), ("pm", [128], H), ("pmth", [128], H), ("pmt", [128], f32), ("pt", [4, 128], H), ("idh", [128], H),
+    ("idb", [128], bf), ("nidb", [128], bf), ("ez", [144], H), ("m8", [8], f32), ("m8s", [8], f32), ("hz", [56], bf),
+    ("oz", [56], bf), ("jm", [8], bf), ("oh", [32], f32), ("dn", [272], f32))}
+for _s, _L in enumerate(LS):
+    _R = _L // 16
+    for _n, _sh, _d in (("vu", [2 * _R], u16_), ("w16", [_R], u16_), ("nb16", [_L], u16_), ("ur", [_L], f32), ("mk", [_L], bf),
+                        ("pr", [_L], H), ("nbf", [_L], H), ("nbt", [_L // 32, 2, 16], H), ("wf", [_R], f32), ("xw", [_L], bf),
+                        ("xg", [16 * _L], bf), ("cz", [32 * _L + 32], bf), ("s1", [_R * 17], f32), ("s2", [_R * 17], f32),
+                        ("s3", [_R * 17], f32), ("sm", [12, _R], H), ("gi", [2, _R], i32), ("sg", [_L], bf),
+                        ("xv", [4, _L], bf), ("ld", [4, _L], bf)):
+        SCRATCH["%s%d" % (_n, _s)] = ("sbuf", [128] + _sh, _d)
+NB_ = 8 // NS
+for _b in range(NB_ * NS):
+    SCRATCH["ps%d" % _b] = ("psum", [128, 16, 32] if _b % NB_ == 0 else [128, 512], f32)
+SEMAPHORES = ["V", "S", "P", "G", "loc"] + ["d%d" % i for i in range(24)] + ["a%d" % i for i in range(4 * NS)]
+
+
+def build():
+    ops = []
+    last_w, readers, bank_last = {}, {}, {}
+    nd = [0]
+    tag = ["i", 0]
+
+    def op(eng, cost, fn, r=(), w=(), banks=(), lat=0.0, kind="c", n=1):
+        i = len(ops)
+        deps, soft = set(), set()
+        for k in r:
+            if k in last_w: deps.add(last_w[k])
+        for k in w:
+            if k in last_w: deps.add(last_w[k])
+            deps.update(readers.get(k, ()))
+        for b in banks: soft.update(bank_last.get(b, ()))
+        for k in r: readers.setdefault(k, []).append(i)
+        for k in w:
+            last_w[k] = i; readers[k] = []
+        for b in banks:
+            prev = bank_last.get(b, [])
+            if prev and ops[prev[-1]]["eng"] == eng: prev.append(i)
+            else: bank_last[b] = [i]
+        bdeps = set(j for j in soft if ops[j]["eng"] != eng)
+        for j in soft:
+            if ops[j]["eng"] == eng: bdeps.update(ops[j]["bdeps"])
+        deps.update(bdeps)
+        deps.discard(i)
+        tag[1] += 1
+        o = {"eng": eng, "cost": cost, "fn": fn, "deps": deps, "bdeps": bdeps, "lat": lat, "kind": kind, "n": n, "tag": tuple(tag)}
+        if kind == "d":
+            o["sem"] = "d%d" % nd[0]; nd[0] += 1
+        ops.append(o)
+        return i
+
+    def V(n, fn, r, w, banks=(), f=1.0): return op("V", (max(64.0, n * f), 0, 0, 0), fn, r, w, banks)
+    def S(n, fn, r, w, banks=()): return op("S", (max(64.0, n), 0, 0, 0), fn, r, w, banks)
+    def X(e, n, fn, r, w): return op(e, (60.0, n, 0, 18.0), fn, r, w)
+    def P(c, fn, r, w, banks): return op("P", (0, 0, c, 0), fn, r, w, banks)
+    def G(n, fn, r, w): return op("G", (160.0 + 2 * n, 0, 0, 0), fn, r, w)
+    def D(q, lat, fn, r, w, n=1): return op(q, (60.0 * n, 0, 0, 0), fn, r, w, lat=1800.0 + lat, kind="d", n=n)
+
+    def mms(lst):
+        def fn(g, T, e):
+            ins = None
+            for o, l, r, a, b in lst(T): ins = g.tensor.matmul(o, l, r, a, b)
+            return ins
+        return fn
+    def grp(o, prs, first=True, last=True): return [(o, l, r, first and i == 0, last and i == len(prs) - 1) for i, (l, r) in enumerate(prs)]
+    def ts(o, i, s1, s2, o0, o1=None):
+        def fn(g, T, e):
+            a = s1(T) if not isinstance(s1, (int, float)) else s1
+            if o1 is None: return g.vector.tensor_scalar(o(T), i(T), a, None, o0)
+            return g.vector.tensor_scalar(o(T), i(T), a, s2, o0, o1)
+        return fn
+    def tt(o, a, b, o0): return lambda g, T, e: g.vector.tensor_tensor(o(T), a(T), b(T), o0)
+    def cp(o, a): return lambda g, T, e: g.vector.tensor_copy(o(T), a(T))
+    def act(o, a, f=None, **kw): return lambda g, T, e: g.scalar.activation(o(T), a(T), F.Identity if f is None else f, **kw)
+    def ms(o, c): return lambda g, T, e: g.vector.memset(o(T), c)
+    def scan(o, a, b, o0, o1): return lambda g, T, e: g.vector.tensor_tensor_scan(o(T), a(T), b(T), 0.0, o0, o1)
+    def B(name, *ix): return lambda T: T[name][ix] if ix else T[name][:]
+    def C(name, a, b, st=None): return lambda T: T[name][:, a:b:st]
+    def ind(win, off): return lambda T: T[win][:].indirect(off(T))
+    def io(name, n, pat, base, cm):
+        kw = {} if SCRATCH[name][2] == i32 else {"allow_small_or_imprecise_dtypes": True}
+        G(n, lambda g, T, e: g.iota(T[name][:], pat, base, cm, **kw), [], [name])
+    al = slice(None)
+    EQ = A.is_equal
+
+    D("Y", 5300, lambda g, T, e: [g.sync.dma_start(T.adjs[:], T.adj[:])], [], ["adjs"])
+    D("S", 300, lambda g, T, e: [g.scalar.dma_start(T.v0s[:], T.v0[:]), g.scalar.dma_start(T.j0s[:], T.j0[:])], [], ["v0s", "j0s"], n=2)
+    D("Y", 7900, lambda g, T, e: [g.sync.dma_start(T.xs[:], T.x[:])], [], ["xs"])
+    D("Y", 8300, lambda g, T, e: [g.sync.dma_start(T.cs[:], T.c0[:])], [], ["c%d" % s for s in range(NS)])
+    D("Y", 8600, lambda g, T, e: [g.sync.dma_start(T.y0s[:], T.y0[:]), g.sync.dma_start(T.hs[:, 0:1], T.h[:])], [], ["y0s", "hs"], n=2)
+    io("io1", 16, [[-1, 16]], 16, 1)
+    io("ie", 144, [[-1, 144]], 15, 1)
+    io("idn", 128, [[-1, 128]], 0, 1)
+    io("ib", 128, [[-1, 16], [-16, 8]], 0, 1)
+    io("im", 8, [[-16, 8]], 0, 1)
+    io("ic", 128, [[-1, 16], [-32, 4], [1000, 2]], 0, 1)
+    io("ia", 128, [[-1, 8], [-8, 16]], 0, 1)
+    io("i16", 16, [[1, 16]], 0, 16)
+    io("i512", 512, [[1, 512]], 0, 0)
+    io("adjd", 2048, [[-1, 2048]], 0, 0)
+    D("G", 5300, lambda g, T, e: [g.dma_start(T.adjd[:], T.adj[:], accum_op=A.add)], ["adjs"], ["adjd"])
+    D("Y", 5300, lambda g, T, e: [g.sync.dma_start(T.adjp[16 * k + 1:16 * k + 16, :], T.adj[16 * k:16 * k + 15, :]) for k in range(8)]
+      + [g.sync.dma_start(T.adjp[16 * k:16 * k + 1, :], T.i16[:]) for k in range(8)], ["i16", "xs"], ["adjp"], n=16)
+    IDT = ["idt%d" % k for k in range(4)]
+    for k in range(4): S(512, act(C("idt", 512 * k, 512 * k + 512), B("i512"), bias=float(512 * k)), ["i512"], [IDT[k]])
+    V(16, ts(B("io2"), B("io1"), 15, None, A.bitwise_and), ["io1"], ["io2"])
+    V(16, ms(C("oh", 16, 32), 0.0), [], ["oh1"])
+    V(16, ts(C("oh", 0, 16), B("io2"), 0.0, None, EQ), ["io2"], ["oh0"])
+    V(16, cp(C("imf", 0, 1), C("io2", 0, 1)), ["io2"], ["pmod"])
+    V(144, ts(B("ez"), B("ie"), C("imf", 0, 1), None, EQ), ["ie", "pmod"], ["ez"])
+    for a, b in (("idh", "idn"), ("pmth", "ib"), ("pmt", "ib"), ("pm", "ia"), ("idb", "idn")):
+        V(128, ts(B(a), B(b), 0.0, None, EQ), [b], [a])
+    V(128, ts(B("nidb"), B("idn"), 0.0, -1.0, EQ, A.mult), ["idn"], ["nidb"])
+    V(8, ts(B("im2"), B("im"), 4, None, A.arith_shift_right), ["im"], ["im2"])
+    V(8, ts(B("m8"), B("im2"), 0.0, None, EQ), ["im2"], ["m8"])
+    V(8, ts(B("m8s"), B("im2"), 0.0, SC, EQ, A.mult), ["im2"], ["m8s"])
+    PT = ["pt%d" % k for k in range(4)]
+    for k in range(4): V(128, ts(B("pt", al, k, al), B("ic"), float(16 * (k // 2)) + 1000.0 * (k % 2), None, EQ), ["ic"], [PT[k]])
+    V(56, ms(B("hz"), 0.0), [], ["hz"])
+    V(8, ts(C("hz", 24, 32), B("m8"), C("hs", 0, 1), None, A.mult), ["m8", "hs"], ["hz"])
+    V(56, ms(B("oz"), 0.0), [], ["oz"])
+    V(8, cp(C("oz", 24, 32), B("m8s")), ["m8s"], ["oz"])
+    V(8, ts(C("imf", 1, 2), C("imf", 0, 1), -16.0, None, A.add), ["pmod"], ["pm16"])
+    V(8, ts(B("jm"), B("m8"), C("imf", 1, 2), None, A.mult), ["m8", "pm16"], ["jm"])
+    V(17 * max(LS) // 16, ms(C("dn", 0, 17 * max(LS) // 16), 4096.0), [], ["dn"])
+    V(16, ms(C("dn", 0, 17 * max(LS) // 16, 17), -float(2 ** 31)), [], ["dn"])
+    V(16, cp(B("j16"), B("j0s")), ["j0s"], ["j16"])
+    V(16, cp(B("v0h"), B("v0s")), ["v0s"], ["v0h"])
+    V(16, ts(B("b0h"), B("j0s"), 16.0, None, A.is_ge), ["j0s"], ["b0h"])
+    V(16, tt(B("bv0"), B("b0h"), B("v0h"), A.mult), ["b0h", "v0h"], ["bv0"])
+
+    def stream(s):
+        L, l0 = LS[s], L0[s]
+        R, k0 = L // 16, l0 // 16
+        n = lambda x: "%s%d" % (x, s)
+        N = lambda *x: [n(y) for y in x]
+        bN = NB_ * s
+        bK, bW, bE = (bN + 1, bN + 2, bN + 3) if NB_ == 4 else (bN + 1, bN + 1, bN + 1)
+        oW, oE = 136, 184
+        pK, pN, pW, pE = ["ps%d" % b for b in (bK, bN, bW, bE)]
+        kp = C(pK, 0, 17 * R); nb = B(pN, al, slice(0, R), slice(0, 17)); nb0 = B(pN, al, slice(0, R), 0)
+        VP, WP, VU, AG = C(pW, oW, oW + 2 * R), C(pW, oW + 32, oW + 32 + R), C(pE, oE, oE + R), C(pE, oE + 16, oE + 16 + R)
+        DP, CP = C(pE, oE + 32, oE + 32 + L), C(pE, oE + 32 + L, oE + 32 + 2 * L)
+        JP = B(pK, slice(0, 8), slice(0, L))
+        v_, d_, b_, ag_, bq_, a1_, e_, eq_, t1_, t2_, t3_, an_ = [B(n("sm"), al, j, al) for j in range(12)]
+        cS = C("cs", l0, l0 + L)
+        v16, u16, w16 = C(n("vu"), 0, R), C(n("vu"), R, 2 * R), B(n("w16"))
+        NP = (L + PIECE - 1) // PIECE
+        pk = lambda x: [n(x) + "_%d" % j for j in range(NP)]
+        CZ = [n("cz") + "_%d" % q for q in range(8)]
+
+        def stations(more):
+            for q in range(8):
+                V(L, ts(C(n("cz"), 24 + q, 32 * L, 32), cS, C("m8s", q, q + 1), None, A.mult), [n("c"), "m8s"] + more, [CZ[q]], f=0.5)
+
+        def to_u(T, ps, a, b, st, z, y):
+            return sum([grp(T[ps][32 * q:32 * q + 32, a:b:st], [(T[z][:, 24 - 8 * c:56 - 8 * c], y(T)[:, 4 * q + c::16]) for c in range(4)]) for q in range(4)], [])
+
+        def again(y, ykey):
+            P(512, mms(lambda T: to_u(T, pE, oE + 16, oE + 16 + R, None, "hz", y)), [ykey, "hz"], N("AG"), [bE])
+            V(R, cp(B(n("gi"), al, 0, al), AG), N("AG"), N("gi0"), [bE])
+            V(R, ts(B(n("gi"), al, 1, al), B(n("gi"), al, 0, al), 2047, None, A.bitwise_and), N("gi0"), N("gi1"))
+            V(R, cp(an_, B(n("gi"), al, 1, al)), N("gi1"), N("an"))
+
+        def masks():
+            X("S", L, act(B(n("ur")), ind("idt", u16)), IDT + N("vu"), N("ur"))
+            X("V", L, tt(B(n("mk")), ind("adjp", v16), B(n("ur")), EQ), ["adjp"] + N("vu", "ur"), N("mk"))
+
+        tag[0] = ("i", s); tag[1] = 0
+        zs = []
+        for a in range(0, 32 * L + 32, 528):
+            zs.append(n("z") + str(a)); b = min(a + 528, 32 * L + 32)
+            V(b - a, ms(C(n("cz"), a, b), 0.0), [], [zs[-1]], f=0.5)
+        V(R, cp(v16, C("v0s", k0, k0 + R)), ["v0s"], N("vu"))
+        stations(zs)
+        again(C("y0s", l0, l0 + L), "y0s")
+        P(64, mms(lambda T: grp(VU(T), [(T.pmth[:], T.v0h[:, k0:k0 + R])])), ["pmth", "v0h"], N("VU"), [bE])
+        V(R, cp(v_, VU), N("VU"), N("v"), [bE])
+        X("S", L, act(B(n("mk")), ind("oh", C("j16", k0, k0 + R))), ["oh0", "oh1", "j16"], N("mk"))
+        yield
+
+        for t in range(1, STEPS + 1):
+            tag[0] = (s, t); tag[1] = 0
+            tab = "adjs" if t == 1 else "adjd"
+            if t > 1: masks()
+            X("V", L, tt(B(n("pr")), ind(tab, v16), B(n("mk")), A.mult), [tab] + N("vu", "mk"), N("pr"))
+            if t == 1: P(64, mms(lambda T: grp(WP(T), [(T.idh[:], T.bv0[:, k0:k0 + R])], True, False)), ["idh", "bv0"], N("WP"), [bW])
+            P(1024, mms(lambda T: grp(WP(T), [(T.ez[:, 15 - j:143 - j], T[n("pr")][:, j::16]) for j in range(16)], False, True)), ["ez", n("pr")], N("WP"), [bW])
+            V(R, cp(w16, WP), N("WP"), N("w16"), [bW])
+            X("V", L, cp(B(n("nb16")), ind("adjs", w16)), ["adjs", n("w16")], N("nb16"))
+            X("V", L, tt(B(n("xw")), ind("xs", w16), cS, A.mult), ["xs"] + N("w16", "c"), N("xw"))
+            P(512, mms(lambda T: to_u(T, pK, 0, 17 * R, 17, "oz", B(n("xw")))), ["oz", n("xw")], N("K0"), [bK])
+            S(R, act(B(n("wf")), WP), N("WP"), N("wf"), [bW])
+            V(L, cp(B(n("nbf")), B(n("nb16"))), N("nb16"), N("nbf"), f=0.5)
+            V(L, lambda g, T, e: g.vector.transpose(T[n("nbt")][:], T[n("nbf")][:]), N("nbf"), N("nbt"), f=0.5)
+            P(512, mms(lambda T: grp(nb0(T), [(T.pmt[:], T[n("wf")][:])]) + sum(
+                [grp(T[pN][:, c:R:2, 1:17], [(T.pt[:, 2 * c + z, :], T[n("nbt")][:, :, z, :]) for z in range(2)]) for c in range(2)], [])),
+              ["pmt"] + N("wf", "nbt") + PT, N("NB"), [bN])
+            V(R, tt(d_, nb0, v_, A.subtract), N("NB", "v"), N("d"), [bN])
+            V(R, ts(b_, d_, 0.0, None, EQ), N("d"), N("b"))
+            V(R, tt(ag_, an_, v_, A.subtract), N("an", "v"), N("ag"))
+            V(R, tt(bq_, b_, ag_, A.mult), N("b", "ag"), N("bq"))
+            V(R, tt(a1_, d_, bq_, A.add), N("d", "bq"), N("a1"))
+            for j in range(NP):
+                a, b = j * PIECE, min(L, (j + 1) * PIECE)
+                def big(g, T, e, a=a, b=b):
+                    o = T[n("xg")][:, 16 * a:16 * b]; i = T.xs[:].indirect(T[n("nb16")][:, a:b])
+                    return g.vector.tensor_copy(o, i) if e == "V" else g.scalar.activation(o, i, F.Identity)
+                i = X("F", 16 * (b - a), big, ["xs", n("nb16")], [pk("xg")[j]])
+                ops[i]["fix"] = "V" if j >= NP - NV else "S"
+                P(32 * (b - a), mms(lambda T, a=a, b=b: [
+                    (T[pK][32 * (m % 16 // 4):32 * (m % 16 // 4) + 32, 17 * (m // 16) + 1:17 * (m // 16) + 17],
+                     T[n("cz")][:, 32 * m + 24 - 8 * (m % 4):32 * m + 56 - 8 * (m % 4)],
+                     T[n("xg")][:, 16 * m:16 * m + 16], m % 4 == 0, m % 4 == 3) for m in range(a, b)]),
+                  CZ + [pk("xg")[j]], [pk("KP")[j]], [bK])
+            s1, s2, s3 = B(n("s1")), B(n("s2")), B(n("s3"))
+            V(17 * R, scan(s1, C("dn", 0, 17 * R), kp, A.add, A.max), pk("KP") + ["dn", n("K0")], N("s1"), [bK])
+            V(17 * R, tt(s2, s1, kp, A.subtract), pk("KP") + N("s1", "K0"), N("s2"), [bK])
+            V(17 * R, tt(s3, nb, s2, A.subtract), N("NB", "s2"), N("s3"), [bN])
+            V(17 * R, scan(s1, s2, s3, A.min, A.max), N("s2", "s3"), N("s1"))
+            p_ = C(n("s1"), 16, 17 * R, 17)
+            V(R, tt(eq_, p_, v_, EQ), N("s1", "v"), N("eq"))
+            V(R, tt(e_, p_, v_, A.subtract), N("s1", "v"), N("e"))
+            V(R, tt(t2_, eq_, a1_, A.mult), N("eq", "a1"), N("t2"))
+            V(R, tt(t1_, e_, b_, A.mult), N("e", "b"), N("t1"))
+            V(R, tt(t3_, eq_, bq_, A.mult), N("eq", "bq"), N("t3"))
+            tv = lambda T, m: [(T[m][:], v_(T)), (T[m][:], t1_(T)), (T[m][:], t2_(T))]
+            P(384, mms(lambda T: grp(T[pW][:, oW:oW + R], tv(T, "pm")) + grp(T[pW][:, oW + R:oW + 2 * R], [(T.pm[:], v_(T)), (T.pm[:], d_(T)), (T.pm[:], t3_(T))])),
+              ["pm"] + N("v", "d", "t1", "t2", "t3"), N("VP"), [bW])
+            V(2 * R, cp(B(n("vu")), VP), N("VP"), N("vu"), [bW])
+            if t < STEPS:
+                P(192, mms(lambda T: grp(VU(T), tv(T, "idh"))), ["idh"] + N("v", "t1", "t2"), N("VU"), [bE])
+                P(192, mms(lambda T: grp(WP(T), tv(T, "pm"), True, False)), ["pm"] + N("v", "t1", "t2"), N("WP"), [bW])
+                V(R, cp(v_, VU), N("VU"), N("v"), [bE])
+            if t % 2 == 0:
+                x = t // 2 - 1
+                xv, ld, kx, kl = B(n("xv"), al, x, al), B(n("ld"), al, x, al), n("xv") + str(x), n("ld") + str(x)
+                X("S", L, act(xv, ind("xs", v16)), ["xs", n("vu")], [kx])
+                sd = op("G", (300.0, 0, 0, 0), (n("ld"), n("xv"), x, "a%d" % (4 * s + x)), [kx], [], kind="r")
+                rv = op("R", (0, 0, 0, 0), None, [], [kl], lat=2000.0, kind="a")
+                ops[rv]["deps"].add(sd); ops[rv]["sem"] = "a%d" % (4 * s + x)
+                P(2 * L, mms(lambda T, xv=xv, ld=ld: grp(DP(T), [(T.nidb[:], xv(T)), (T.idb[:], ld(T))])), ["idb", "nidb", kx, kl], N("DP"), [bE])
+                S(L, act(B(n("sg")), DP, F.Sign), N("DP"), N("sg"), [bE])
+                P(2 * L, mms(lambda T: grp(CP(T), [(T.idb[:], cS(T)), (T.idb[:], T[n("sg")][:])])), ["idb"] + N("c", "sg"), N("CP"), [bE])
+                if t < STEPS:
+                    V(L, ts(cS, CP, 15.0, -15.0, A.min, A.max), N("CP"), N("c"), [bE])
+                    stations([])
+                    again(ld, kl)
+                else:
+                    co, vr = C("cof", l0, l0 + L), C("vr", l0, l0 + L)
+                    V(L, ts(co, CP, 15.0, -15.0, A.min, A.max), N("CP"), N("co"), [bE])
+                    D("Y", 300, lambda g, T, e: [g.sync.dma_start(T.co[:, l0:l0 + L], co(T))], N("co"), [])
+                    masks()
+                    P(L, mms(lambda T: grp(JP(T), [(T.jm[:], T[n("mk")][:])])), ["jm", n("mk")], N("JP", "K0") + pk("KP"), [bK])
+                    S(L, act(lambda T: T.jr[0:8, l0:l0 + L], JP, bias=16.0), N("JP"), N("jr"), [bK])
+                    D("Y", 100, lambda g, T, e: [g.sync.dma_start(T.jo[:, l0:l0 + L], T.jr[0:8, l0:l0 + L])], N("jr"), [])
+                    X("S", L, act(vr, ind("idt", v16)), IDT + N("vu"), N("vr"))
+                    D("Y", 100, lambda g, T, e: [g.sync.dma_start(T.vo[:, l0:l0 + L], T.vr[0:128:16, l0:l0 + L])], N("vr"), [])
+            yield
+
+    gens = [stream(s) for s in range(NS)]
+    for t in range(STEPS + 1):
+        for x in gens: next(x)
+    return ops
+
+
+def cost(o, e, m):
+    c = o["cost"]
+    return c[0] + m[0] * c[1] + m[2] * c[2] + (c[3] if e == "S" else 0.0) + (m[3] if e in "VS" else 0.0)
+
+
+def place(ops, order, on, m):
+    free = dict.fromkeys("VSPGYR", 0.0); fin = [0.0] * len(ops)
+    for i in order:
+        o = ops[i]; e = on[i]; t = free[e]
+        for d in o["deps"]:
+            if fin[d] > t: t = fin[d]
+        t += cost(o, e, m); free[e] = t
+        fin[i] = t + o["lat"] + m[1]
+    return max(fin)
+
+
+def fit(key, pred, succ, cs, lat, on, back):
+    n = len(key)
+    if back: pred, succ = succ, pred
+    left = [len(p) for p in pred]; rd = [i for i in range(n) if not left[i]]
+    busy = {e: ([], []) for e in "VSPGYR"}; st = [0.0] * n; fi = [0.0] * n
+    while rd:
+        i = min(rd, key=lambda j: key[j])
+        rd.remove(i)
+        t = 0.0
+        for j in pred[i]:
+            z = fi[j] + (lat[i] if back else lat[j])
+            if z > t: t = z
+        if back and not pred[i]: t = lat[i]
+        c = cs[i][on[i]]; a, b = busy[on[i]]; k = len(b)
+        while k and b[k - 1] > t: k -= 1
+        while k < len(a) and a[k] < t + c:
+            t = max(t, b[k]); k += 1
+        a.insert(k, t); b.insert(k, t + c); st[i] = t; fi[i] = t + c
+        for j in succ[i]:
+            left[j] -= 1
+            if not left[j]: rd.append(j)
+    return st, fi
+
+
+def search(ops):
+    n = len(ops); m = MODELS[0]
+    pred = [sorted(o["deps"]) for o in ops]
+    succ = [[] for _ in ops]
+    for i in range(n):
+        for d in pred[i]: succ[d].append(i)
+    cs = [{e: cost(o, e, m) for e in ("SV" if o["eng"] == "F" else o["eng"])} for o in ops]
+    lat = [o["lat"] + m[1] for o in ops]
+    on = [o.get("fix", o["eng"]) for o in ops]
+    flex = [i for i in range(n) if ops[i]["eng"] == "F"]
+    base = [0.0] * n
+    for i in range(n - 1, -1, -1): base[i] = cs[i][on[i]] + lat[i] + max([base[j] for j in succ[i]] + [0.0])
+    seed = [12345]
+    def rnd():
+        seed[0] = (seed[0] * 6364136223846793005 + 1442695040888963407) % (1 << 64)
+        return (seed[0] >> 33) / float(1 << 31)
+    def sid(o): return o["tag"][0][0] if isinstance(o["tag"][0][0], int) else 0
+    key = [-base[i] + 7000.0 / NS * sid(ops[i]) for i in range(n)]
+    best = cur = None
+    for it in range(ITER):
+        for r in range(2):
+            for i in range(5): key[i] = -1e9 + i
+            st, fi = fit(key, pred, succ, cs, lat, on, False)
+            order = sorted(range(n), key=lambda i: (st[i], i))
+            sc = sum(place(ops, order, on, q) for q in MODELS) / len(MODELS)
+            if cur is None or sc < cur[0] + 120.0 * (1.0 - it / float(ITER)): cur = (sc, order, list(on), st)
+            if best is None or sc < best[0]: best = (sc, order, list(on), st)
+            key = [-x for x in fit([-(fi[i] + lat[i]) for i in range(n)], pred, succ, cs, lat, on, True)[1]]
+        c = rnd() * cur[0]; w = (2000.0, 6000.0, 1e5)[int(rnd() * 3)]; a = (200.0, 800.0, 2000.0)[int(rnd() * 3)]
+        key = [x + ((rnd() - 0.5) * a if abs(x - c) < w else 0.0) for x in cur[3]]
+        on = list(cur[2])
+        if rnd() < 0.5:
+            i = flex[int(rnd() * len(flex))]; on[i] = "V" if on[i] == "S" else "S"
+    return best
+
+
+PLAN = {}
+
+
+def plan():
+    if not PLAN:
+        ops = build()
+        sc, order, on, st = search(ops)
+        cnt = dict.fromkeys("VSPG", 0)
+        known = {e: {} for e in "VSPGY"}
+        total = {}
+        for i in order:
+            o = ops[i]; e = o["on"] = on[i]; o["st"] = st[i]
+            if o["kind"] == "a":
+                o["sig"] = (o["sem"], NENG); o["clock"] = {o["sem"]: NENG}; total[o["sem"]] = NENG
+                continue
+            waits = []
+            kn = known[e]
+            for d in sorted(o["deps"], key=lambda j: -ops[j]["st"]):
+                sem, c = ops[d]["sig"]
+                if (e == "P" and sem == "P") or kn.get(sem, 0) >= c: continue
+                waits.append((sem, c))
+                for k, v in ops[d]["clock"].items():
+                    if kn.get(k, 0) < v: kn[k] = v
+            o["waits"] = waits
+            if o["kind"] == "d": o["sig"] = (o["sem"], 16 * o["n"])
+            elif o["kind"] == "r": o["sig"] = ("loc", total.get("loc", 0) + NENG)
+            else:
+                cnt[e] += 1; o["sig"] = (e, cnt[e])
+            total[o["sig"][0]] = o["sig"][1]
+            o["clock"] = dict(kn); o["clock"][o["sig"][0]] = o["sig"][1]
+        PLAN["ops"] = ops; PLAN["order"] = order; PLAN["total"] = total; PLAN["on"] = on
+    return PLAN
+
+
+def rank_program(g, core, T, topo):
+    rank = T.rank_of(core)
+    if rank is None:
+        return
+    pl = plan()
+    nxt = T.cores[(rank + 1) % len(T.cores)]
+    rid, pid = topo.addr(nxt)[:2]
+    mask = sum(1 << e for e in topo.engines(core, nxt)[:NENG])
+    q = {"V": g.vector, "S": g.scalar, "P": g.tensor, "G": g, "Y": g.sync}
+    for i in pl["order"]:
+        o = pl["ops"][i]
+        if o["kind"] == "a": continue
+        e = o["on"]
+        for sem, c in o["waits"]: q[e].wait_ge(T.sem[sem], c)
+        if o["kind"] == "r":
+            ld, xv, x, sem = o["fn"]
+            g.remote_dma(T[ld][:, x, :], T[xv][:, x, :], T.sem[sem], T.sem["loc"], pid, rid, mask)
+        elif o["kind"] == "d":
+            for ins in o["fn"](g, T, e): ins.then_inc(T.sem[o["sem"]], 16)
+        else:
+            o["fn"](g, T, e).then_inc(T.sem[e], 1)
+    for sem, c in pl["total"].items():
+        g.wait_ge(T.sem[sem], c)

@@ -2,11 +2,11 @@ from concourse.mybir import AluOpType as A, ActivationFunctionType as F
 
 LS = [128, 128]
 PIECE = 16
-NV = 2
+NV = 1
 H = "float16"
 NENG = 8
-MODELS = [(1.56, 100.0, 0.5, 0.0), (1.2, 150.0, 0.5, 20.0), (1.9, 60.0, 0.6, 0.0)]
-ITER = 900
+MODELS = [(1.56, 150.0, 0.4, 40.0), (1.2, 120.0, 0.5, 40.0), (2.0, 100.0, 0.35, 40.0)]
+ITER = 1600
 STEPS = 8
 NS = len(LS)
 L0 = [sum(LS[:i]) for i in range(NS)]
@@ -20,19 +20,19 @@ SCRATCH = {k: ("sbuf", [128] + sh, d) for k, sh, d in (
     ("cof", [256], f32), ("vr", [256], f32), ("jr", [256], f32), ("ia", [128], f32), ("ib", [128], f32), ("ic", [128], f32),
     ("idn", [128], f32), ("ie", [144], i32), ("im", [8], i32), ("im2", [8], i32), ("imf", [8], f32), ("io1", [16], i32),
     ("io2", [16], i32), ("pm", [128], H), ("pmth", [128], H), ("pmt", [128], f32), ("pt", [4, 128], H), ("idh", [128], H),
+    ("nidh", [128], H), ("idf", [128], f32),
     ("idb", [128], bf), ("nidb", [128], bf), ("ez", [144], H), ("m8", [8], f32), ("m8s", [8], f32), ("hz", [56], bf),
-    ("oz", [56], bf), ("jm", [8], bf), ("oh", [32], f32), ("dn", [272], f32))}
+    ("oz", [56], bf), ("jm", [8], bf), ("oh", [32], f32), ("dn", [136], f32))}
 for _s, _L in enumerate(LS):
     _R = _L // 16
     for _n, _sh, _d in (("vu", [2 * _R], u16_), ("w16", [_R], u16_), ("nb16", [_L], u16_), ("ur", [_L], f32), ("mk", [_L], bf),
                         ("pr", [_L], H), ("nbf", [_L], H), ("nbt", [_L // 32, 2, 16], H), ("wf", [_R], f32), ("xw", [_L], bf),
                         ("xg", [16 * _L], bf), ("cz", [32 * _L + 32], bf), ("s1", [_R * 17], f32), ("s2", [_R * 17], f32),
-                        ("s3", [_R * 17], f32), ("sm", [12, _R], H), ("gi", [2, _R], i32), ("sg", [_L], bf),
+                        ("s3", [_R * 17], f32), ("sm", [9, _R], H), ("gi", [2, _R], i32), ("sg", [_L], bf),
                         ("xv", [4, _L], bf), ("ld", [4, _L], bf)):
         SCRATCH["%s%d" % (_n, _s)] = ("sbuf", [128] + _sh, _d)
-NB_ = 8 // NS
-for _b in range(NB_ * NS):
-    SCRATCH["ps%d" % _b] = ("psum", [128, 16, 32] if _b % NB_ == 0 else [128, 512], f32)
+for _b in range(8):
+    SCRATCH["ps%d" % _b] = ("psum", [128, 16, 32] if _b % 4 == 0 else [128, 512], f32)
 SEMAPHORES = ["V", "S", "P", "G", "loc"] + ["d%d" % i for i in range(24)] + ["a%d" % i for i in range(4 * NS)]
 
 
@@ -70,8 +70,8 @@ def build():
         ops.append(o)
         return i
 
-    def V(n, fn, r, w, banks=(), f=1.0): return op("V", (max(64.0, n * f), 0, 0, 0), fn, r, w, banks)
-    def S(n, fn, r, w, banks=()): return op("S", (max(64.0, n), 0, 0, 0), fn, r, w, banks)
+    def V(n, fn, r, w, banks=(), f=1.0): return op("V", (64.0 + (n * f if n * f > 64 else 0.0), 0, 0, 0), fn, r, w, banks)
+    def S(n, fn, r, w, banks=()): return op("S", (64.0 + (n if n > 64 else 0.0), 0, 0, 0), fn, r, w, banks)
     def X(e, n, fn, r, w): return op(e, (60.0, n, 0, 18.0), fn, r, w)
     def P(c, fn, r, w, banks): return op("P", (0, 0, c, 0), fn, r, w, banks)
     def G(n, fn, r, w): return op("G", (160.0 + 2 * n, 0, 0, 0), fn, r, w)
@@ -129,22 +129,25 @@ def build():
     V(16, ts(C("oh", 0, 16), B("io2"), 0.0, None, EQ), ["io2"], ["oh0"])
     V(16, cp(C("imf", 0, 1), C("io2", 0, 1)), ["io2"], ["pmod"])
     V(144, ts(B("ez"), B("ie"), C("imf", 0, 1), None, EQ), ["ie", "pmod"], ["ez"])
-    for a, b in (("idh", "idn"), ("pmth", "ib"), ("pmt", "ib"), ("pm", "ia"), ("idb", "idn")):
+    for a, b in (("idf", "idn"), ("pmt", "ib"), ("pm", "ia"), ("idh", "idn")):
         V(128, ts(B(a), B(b), 0.0, None, EQ), [b], [a])
-    V(128, ts(B("nidb"), B("idn"), 0.0, -1.0, EQ, A.mult), ["idn"], ["nidb"])
+    V(128, cp(B("pmth"), B("pmt")), ["pmt"], ["pmth"])
+    V(128, ts(B("nidh"), B("idh"), -1.0, None, A.mult), ["idh"], ["nidh"], f=0.5)
+    S(128, act(B("idb"), B("idf")), ["idf"], ["idb"])
+    S(128, act(B("nidb"), B("idf"), scale=-1.0), ["idf"], ["nidb"])
     V(8, ts(B("im2"), B("im"), 4, None, A.arith_shift_right), ["im"], ["im2"])
     V(8, ts(B("m8"), B("im2"), 0.0, None, EQ), ["im2"], ["m8"])
-    V(8, ts(B("m8s"), B("im2"), 0.0, SC, EQ, A.mult), ["im2"], ["m8s"])
+    S(8, act(B("m8s"), B("m8"), scale=SC), ["m8"], ["m8s"])
     PT = ["pt%d" % k for k in range(4)]
     for k in range(4): V(128, ts(B("pt", al, k, al), B("ic"), float(16 * (k // 2)) + 1000.0 * (k % 2), None, EQ), ["ic"], [PT[k]])
-    V(56, ms(B("hz"), 0.0), [], ["hz"])
+    S(56, act(B("hz"), C("idn", 0, 56), scale=0.0), ["idn"], ["hz"])
     V(8, ts(C("hz", 24, 32), B("m8"), C("hs", 0, 1), None, A.mult), ["m8", "hs"], ["hz"])
-    V(56, ms(B("oz"), 0.0), [], ["oz"])
-    V(8, cp(C("oz", 24, 32), B("m8s")), ["m8s"], ["oz"])
-    V(8, ts(C("imf", 1, 2), C("imf", 0, 1), -16.0, None, A.add), ["pmod"], ["pm16"])
+    S(56, act(B("oz"), C("idn", 0, 56), scale=0.0), ["idn"], ["oz"])
+    S(8, act(C("oz", 24, 32), B("m8"), scale=SC), ["m8"], ["oz"])
+    S(8, act(C("imf", 1, 2), C("imf", 0, 1), bias=-16.0), ["pmod"], ["pm16"])
     V(8, ts(B("jm"), B("m8"), C("imf", 1, 2), None, A.mult), ["m8", "pm16"], ["jm"])
-    V(17 * max(LS) // 16, ms(C("dn", 0, 17 * max(LS) // 16), 4096.0), [], ["dn"])
-    V(16, ms(C("dn", 0, 17 * max(LS) // 16, 17), -float(2 ** 31)), [], ["dn"])
+    V(136, ms(B("dn"), 4096.0), [], ["dn"])
+    V(16, ms(C("dn", 0, 136, 17), -float(2 ** 31)), [], ["dn"])
     V(16, cp(B("j16"), B("j0s")), ["j0s"], ["j16"])
     V(16, cp(B("v0h"), B("v0s")), ["v0s"], ["v0h"])
     V(16, ts(B("b0h"), B("j0s"), 16.0, None, A.is_ge), ["j0s"], ["b0h"])
@@ -155,15 +158,14 @@ def build():
         R, k0 = L // 16, l0 // 16
         n = lambda x: "%s%d" % (x, s)
         N = lambda *x: [n(y) for y in x]
-        bN = NB_ * s
-        bK, bW, bE = (bN + 1, bN + 2, bN + 3) if NB_ == 4 else (bN + 1, bN + 1, bN + 1)
-        oW, oE = 136, 184
+        bN, bK, bW, bE = range(4 * s, 4 * s + 4)
         pK, pN, pW, pE = ["ps%d" % b for b in (bK, bN, bW, bE)]
-        kp = C(pK, 0, 17 * R); nb = B(pN, al, slice(0, R), slice(0, 17)); nb0 = B(pN, al, slice(0, R), 0)
-        VP, WP, VU, AG = C(pW, oW, oW + 2 * R), C(pW, oW + 32, oW + 32 + R), C(pE, oE, oE + R), C(pE, oE + 16, oE + 16 + R)
-        DP, CP = C(pE, oE + 32, oE + 32 + L), C(pE, oE + 32 + L, oE + 32 + 2 * L)
+        kp = C(pK, 0, 17 * R); nb = B(pN, al, slice(0, R), slice(0, 17))
+        nb0, d_ = B(pN, al, slice(0, R), 0), B(pN, al, slice(0, R), 17)
+        VP, WP, VU, AG, ag_ = C(pW, 0, 2 * R), C(pW, 32, 32 + R), C(pE, 0, R), C(pE, 16, 16 + R), C(pE, 24, 24 + R)
+        DP, CP = C(pE, 32, 32 + L), C(pE, 32 + L, 32 + 2 * L)
         JP = B(pK, slice(0, 8), slice(0, L))
-        v_, d_, b_, ag_, bq_, a1_, e_, eq_, t1_, t2_, t3_, an_ = [B(n("sm"), al, j, al) for j in range(12)]
+        v_, b_, bq_, e_, eq_, t1_, t2_, t3_, an_ = [B(n("sm"), al, j, al) for j in range(9)]
         cS = C("cs", l0, l0 + L)
         v16, u16, w16 = C(n("vu"), 0, R), C(n("vu"), R, 2 * R), B(n("w16"))
         NP = (L + PIECE - 1) // PIECE
@@ -172,13 +174,18 @@ def build():
 
         def stations(more):
             for q in range(8):
-                V(L, ts(C(n("cz"), 24 + q, 32 * L, 32), cS, C("m8s", q, q + 1), None, A.mult), [n("c"), "m8s"] + more, [CZ[q]], f=0.5)
+                def put(g, T, e, q=q):
+                    o = T[n("cz")][:, 24 + q:32 * L:32]
+                    if e == "V": return g.vector.tensor_scalar(o, cS(T), T.m8s[:, q:q + 1], None, A.mult)
+                    return g.scalar.activation(o, cS(T), F.Identity, scale=T.m8s[:, q:q + 1])
+                i = op("F", (64.0, 0, 0, 128.0), put, [n("c"), "m8s"] + more, [CZ[q]])
+                ops[i]["fix"] = "S" if q % 4 == 0 else "V"
 
         def to_u(T, ps, a, b, st, z, y):
             return sum([grp(T[ps][32 * q:32 * q + 32, a:b:st], [(T[z][:, 24 - 8 * c:56 - 8 * c], y(T)[:, 4 * q + c::16]) for c in range(4)]) for q in range(4)], [])
 
         def again(y, ykey):
-            P(512, mms(lambda T: to_u(T, pE, oE + 16, oE + 16 + R, None, "hz", y)), [ykey, "hz"], N("AG"), [bE])
+            P(512, mms(lambda T: to_u(T, pE, 16, 16 + R, None, "hz", y)), [ykey, "hz"], N("AG"), [bE])
             V(R, cp(B(n("gi"), al, 0, al), AG), N("AG"), N("gi0"), [bE])
             V(R, ts(B(n("gi"), al, 1, al), B(n("gi"), al, 0, al), 2047, None, A.bitwise_and), N("gi0"), N("gi1"))
             V(R, cp(an_, B(n("gi"), al, 1, al)), N("gi1"), N("an"))
@@ -189,14 +196,14 @@ def build():
 
         tag[0] = ("i", s); tag[1] = 0
         zs = []
-        for a in range(0, 32 * L + 32, 528):
-            zs.append(n("z") + str(a)); b = min(a + 528, 32 * L + 32)
+        for a in range(0, 32 * L + 32, 1032):
+            zs.append(n("z") + str(a)); b = min(a + 1032, 32 * L + 32)
             V(b - a, ms(C(n("cz"), a, b), 0.0), [], [zs[-1]], f=0.5)
         V(R, cp(v16, C("v0s", k0, k0 + R)), ["v0s"], N("vu"))
         stations(zs)
-        again(C("y0s", l0, l0 + L), "y0s")
         P(64, mms(lambda T: grp(VU(T), [(T.pmth[:], T.v0h[:, k0:k0 + R])])), ["pmth", "v0h"], N("VU"), [bE])
         V(R, cp(v_, VU), N("VU"), N("v"), [bE])
+        again(C("y0s", l0, l0 + L), "y0s")
         X("S", L, act(B(n("mk")), ind("oh", C("j16", k0, k0 + R))), ["oh0", "oh1", "j16"], N("mk"))
         yield
 
@@ -214,14 +221,12 @@ def build():
             S(R, act(B(n("wf")), WP), N("WP"), N("wf"), [bW])
             V(L, cp(B(n("nbf")), B(n("nb16"))), N("nb16"), N("nbf"), f=0.5)
             V(L, lambda g, T, e: g.vector.transpose(T[n("nbt")][:], T[n("nbf")][:]), N("nbf"), N("nbt"), f=0.5)
-            P(512, mms(lambda T: grp(nb0(T), [(T.pmt[:], T[n("wf")][:])]) + sum(
+            P(832, mms(lambda T: grp(nb0(T), [(T.pmt[:], T[n("wf")][:])]) + grp(d_(T), [(T.pmt[:], T[n("wf")][:]), (T.nidh[:], v_(T))]) + sum(
                 [grp(T[pN][:, c:R:2, 1:17], [(T.pt[:, 2 * c + z, :], T[n("nbt")][:, :, z, :]) for z in range(2)]) for c in range(2)], [])),
-              ["pmt"] + N("wf", "nbt") + PT, N("NB"), [bN])
-            V(R, tt(d_, nb0, v_, A.subtract), N("NB", "v"), N("d"), [bN])
-            V(R, ts(b_, d_, 0.0, None, EQ), N("d"), N("b"))
-            V(R, tt(ag_, an_, v_, A.subtract), N("an", "v"), N("ag"))
-            V(R, tt(bq_, b_, ag_, A.mult), N("b", "ag"), N("bq"))
-            V(R, tt(a1_, d_, bq_, A.add), N("d", "bq"), N("a1"))
+              ["pmt", "nidh"] + N("wf", "nbt", "v") + PT, N("NB"), [bN])
+            V(R, ts(b_, d_, 0.0, None, EQ), N("NB"), N("b"), [bN])
+            P(128, mms(lambda T: grp(ag_(T), [(T.idh[:], an_(T)), (T.nidh[:], v_(T))])), ["idh", "nidh"] + N("an", "v"), N("ag"), [bE])
+            V(R, tt(bq_, b_, ag_, A.mult), N("b", "ag"), N("bq"), [bE])
             for j in range(NP):
                 a, b = j * PIECE, min(L, (j + 1) * PIECE)
                 def big(g, T, e, a=a, b=b):
@@ -235,23 +240,24 @@ def build():
                      T[n("xg")][:, 16 * m:16 * m + 16], m % 4 == 0, m % 4 == 3) for m in range(a, b)]),
                   CZ + [pk("xg")[j]], [pk("KP")[j]], [bK])
             s1, s2, s3 = B(n("s1")), B(n("s2")), B(n("s3"))
-            V(17 * R, scan(s1, C("dn", 0, 17 * R), kp, A.add, A.max), pk("KP") + ["dn", n("K0")], N("s1"), [bK])
+            V(17 * R, scan(s1, B("dn"), kp, A.add, A.max), pk("KP") + ["dn", n("K0")], N("s1"), [bK])
             V(17 * R, tt(s2, s1, kp, A.subtract), pk("KP") + N("s1", "K0"), N("s2"), [bK])
             V(17 * R, tt(s3, nb, s2, A.subtract), N("NB", "s2"), N("s3"), [bN])
             V(17 * R, scan(s1, s2, s3, A.min, A.max), N("s2", "s3"), N("s1"))
             p_ = C(n("s1"), 16, 17 * R, 17)
             V(R, tt(eq_, p_, v_, EQ), N("s1", "v"), N("eq"))
             V(R, tt(e_, p_, v_, A.subtract), N("s1", "v"), N("e"))
-            V(R, tt(t2_, eq_, a1_, A.mult), N("eq", "a1"), N("t2"))
+            V(R, tt(t2_, eq_, d_, A.mult), N("eq", "NB"), N("t2"), [bN])
             V(R, tt(t1_, e_, b_, A.mult), N("e", "b"), N("t1"))
             V(R, tt(t3_, eq_, bq_, A.mult), N("eq", "bq"), N("t3"))
-            tv = lambda T, m: [(T[m][:], v_(T)), (T[m][:], t1_(T)), (T[m][:], t2_(T))]
-            P(384, mms(lambda T: grp(T[pW][:, oW:oW + R], tv(T, "pm")) + grp(T[pW][:, oW + R:oW + 2 * R], [(T.pm[:], v_(T)), (T.pm[:], d_(T)), (T.pm[:], t3_(T))])),
-              ["pm"] + N("v", "d", "t1", "t2", "t3"), N("VP"), [bW])
+            tv = lambda T, m: [(T[m][:], y(T)) for y in (v_, t2_, t1_, t3_)]
+            TV = N("v", "t1", "t2", "t3")
+            P(576, mms(lambda T: grp(T[pW][:, R:2 * R], [(T.idf[:], T[n("wf")][:]), (T.pm[:], t3_(T))]) + grp(T[pW][:, 0:R], tv(T, "pm"))),
+              ["pm", "idf", n("wf")] + TV, N("VP"), [bW])
             V(2 * R, cp(B(n("vu")), VP), N("VP"), N("vu"), [bW])
             if t < STEPS:
-                P(192, mms(lambda T: grp(VU(T), tv(T, "idh"))), ["idh"] + N("v", "t1", "t2"), N("VU"), [bE])
-                P(192, mms(lambda T: grp(WP(T), tv(T, "pm"), True, False)), ["pm"] + N("v", "t1", "t2"), N("WP"), [bW])
+                P(256, mms(lambda T: grp(VU(T), tv(T, "idh"))), ["idh"] + TV, N("VU"), [bE])
+                P(256, mms(lambda T: grp(WP(T), tv(T, "pm"), True, False)), ["pm"] + TV, N("WP"), [bW])
                 V(R, cp(v_, VU), N("VU"), N("v"), [bE])
             if t % 2 == 0:
                 x = t // 2 - 1
@@ -342,7 +348,7 @@ def search(ops):
         seed[0] = (seed[0] * 6364136223846793005 + 1442695040888963407) % (1 << 64)
         return (seed[0] >> 33) / float(1 << 31)
     def sid(o): return o["tag"][0][0] if isinstance(o["tag"][0][0], int) else 0
-    key = [-base[i] + 7000.0 / NS * sid(ops[i]) for i in range(n)]
+    key = [-base[i] + 9000.0 / NS * sid(ops[i]) for i in range(n)]
     best = cur = None
     for it in range(ITER):
         for r in range(2):

from concourse.mybir import AluOpType as A, ActivationFunctionType as F

LS = [128, 128]
PIECE = 16
NV = 1
H = "float16"
NENG = 8
MODELS = [(1.56, 150.0, 0.4, 40.0), (1.2, 120.0, 0.5, 40.0), (2.0, 100.0, 0.35, 40.0)]
ITER = 1600
STEPS = 8
NS = len(LS)
L0 = [sum(LS[:i]) for i in range(NS)]
SC = float(2 ** 17)
f32, bf, i32, u16_ = "float32", "bfloat16", "int32", "uint16"

SCRATCH = {k: ("sbuf", [128] + sh, d) for k, sh, d in (
    ("adjs", [2048], i32), ("adjp", [2048], i32), ("adjd", [2048], i32), ("idt", [2048], f32), ("xs", [2048], bf),
    ("i512", [512], f32), ("i16", [16], i32), ("v0s", [16], i32), ("j0s", [16], i32), ("j16", [16], u16_),
    ("v0h", [16], H), ("b0h", [16], H), ("bv0", [16], H), ("cs", [256], bf), ("y0s", [256], bf), ("hs", [8], bf),
    ("cof", [256], f32), ("vr", [256], f32), ("jr", [256], f32), ("ia", [128], f32), ("ib", [128], f32), ("ic", [128], f32),
    ("idn", [128], f32), ("ie", [144], i32), ("im", [8], i32), ("im2", [8], i32), ("imf", [8], f32), ("io1", [16], i32),
    ("io2", [16], i32), ("pm", [128], H), ("pmth", [128], H), ("pmt", [128], f32), ("pt", [4, 128], H), ("idh", [128], H),
    ("nidh", [128], H), ("idf", [128], f32),
    ("idb", [128], bf), ("nidb", [128], bf), ("ez", [144], H), ("m8", [8], f32), ("m8s", [8], f32), ("hz", [56], bf),
    ("oz", [56], bf), ("jm", [8], bf), ("oh", [32], f32), ("dn", [136], f32))}
for _s, _L in enumerate(LS):
    _R = _L // 16
    for _n, _sh, _d in (("vu", [2 * _R], u16_), ("w16", [_R], u16_), ("nb16", [_L], u16_), ("ur", [_L], f32), ("mk", [_L], bf),
                        ("pr", [_L], H), ("nbf", [_L], H), ("nbt", [_L // 32, 2, 16], H), ("wf", [_R], f32), ("xw", [_L], bf),
                        ("xg", [16 * _L], bf), ("cz", [32 * _L + 32], bf), ("s1", [_R * 17], f32), ("s2", [_R * 17], f32),
                        ("s3", [_R * 17], f32), ("sm", [9, _R], H), ("gi", [2, _R], i32), ("sg", [_L], bf),
                        ("xv", [4, _L], bf), ("ld", [4, _L], bf)):
        SCRATCH["%s%d" % (_n, _s)] = ("sbuf", [128] + _sh, _d)
for _b in range(8):
    SCRATCH["ps%d" % _b] = ("psum", [128, 16, 32] if _b % 4 == 0 else [128, 512], f32)
SEMAPHORES = ["V", "S", "P", "G", "loc"] + ["d%d" % i for i in range(24)] + ["a%d" % i for i in range(4 * NS)]


def build():
    ops = []
    last_w, readers, bank_last = {}, {}, {}
    nd = [0]
    tag = ["i", 0]

    def op(eng, cost, fn, r=(), w=(), banks=(), lat=0.0, kind="c", n=1):
        i = len(ops)
        deps, soft = set(), set()
        for k in r:
            if k in last_w: deps.add(last_w[k])
        for k in w:
            if k in last_w: deps.add(last_w[k])
            deps.update(readers.get(k, ()))
        for b in banks: soft.update(bank_last.get(b, ()))
        for k in r: readers.setdefault(k, []).append(i)
        for k in w:
            last_w[k] = i; readers[k] = []
        for b in banks:
            prev = bank_last.get(b, [])
            if prev and ops[prev[-1]]["eng"] == eng: prev.append(i)
            else: bank_last[b] = [i]
        bdeps = set(j for j in soft if ops[j]["eng"] != eng)
        for j in soft:
            if ops[j]["eng"] == eng: bdeps.update(ops[j]["bdeps"])
        deps.update(bdeps)
        deps.discard(i)
        tag[1] += 1
        o = {"eng": eng, "cost": cost, "fn": fn, "deps": deps, "bdeps": bdeps, "lat": lat, "kind": kind, "n": n, "tag": tuple(tag)}
        if kind == "d":
            o["sem"] = "d%d" % nd[0]; nd[0] += 1
        ops.append(o)
        return i

    def V(n, fn, r, w, banks=(), f=1.0): return op("V", (64.0 + (n * f if n * f > 64 else 0.0), 0, 0, 0), fn, r, w, banks)
    def S(n, fn, r, w, banks=()): return op("S", (64.0 + (n if n > 64 else 0.0), 0, 0, 0), fn, r, w, banks)
    def X(e, n, fn, r, w): return op(e, (60.0, n, 0, 18.0), fn, r, w)
    def P(c, fn, r, w, banks): return op("P", (0, 0, c, 0), fn, r, w, banks)
    def G(n, fn, r, w): return op("G", (160.0 + 2 * n, 0, 0, 0), fn, r, w)
    def D(q, lat, fn, r, w, n=1): return op(q, (60.0 * n, 0, 0, 0), fn, r, w, lat=1800.0 + lat, kind="d", n=n)

    def mms(lst):
        def fn(g, T, e):
            ins = None
            for o, l, r, a, b in lst(T): ins = g.tensor.matmul(o, l, r, a, b)
            return ins
        return fn
    def grp(o, prs, first=True, last=True): return [(o, l, r, first and i == 0, last and i == len(prs) - 1) for i, (l, r) in enumerate(prs)]
    def ts(o, i, s1, s2, o0, o1=None):
        def fn(g, T, e):
            a = s1(T) if not isinstance(s1, (int, float)) else s1
            if o1 is None: return g.vector.tensor_scalar(o(T), i(T), a, None, o0)
            return g.vector.tensor_scalar(o(T), i(T), a, s2, o0, o1)
        return fn
    def tt(o, a, b, o0): return lambda g, T, e: g.vector.tensor_tensor(o(T), a(T), b(T), o0)
    def cp(o, a): return lambda g, T, e: g.vector.tensor_copy(o(T), a(T))
    def act(o, a, f=None, **kw): return lambda g, T, e: g.scalar.activation(o(T), a(T), F.Identity if f is None else f, **kw)
    def ms(o, c): return lambda g, T, e: g.vector.memset(o(T), c)
    def scan(o, a, b, o0, o1): return lambda g, T, e: g.vector.tensor_tensor_scan(o(T), a(T), b(T), 0.0, o0, o1)
    def B(name, *ix): return lambda T: T[name][ix] if ix else T[name][:]
    def C(name, a, b, st=None): return lambda T: T[name][:, a:b:st]
    def ind(win, off): return lambda T: T[win][:].indirect(off(T))
    def io(name, n, pat, base, cm):
        kw = {} if SCRATCH[name][2] == i32 else {"allow_small_or_imprecise_dtypes": True}
        G(n, lambda g, T, e: g.iota(T[name][:], pat, base, cm, **kw), [], [name])
    al = slice(None)
    EQ = A.is_equal

    D("Y", 5300, lambda g, T, e: [g.sync.dma_start(T.adjs[:], T.adj[:])], [], ["adjs"])
    D("S", 300, lambda g, T, e: [g.scalar.dma_start(T.v0s[:], T.v0[:]), g.scalar.dma_start(T.j0s[:], T.j0[:])], [], ["v0s", "j0s"], n=2)
    D("Y", 7900, lambda g, T, e: [g.sync.dma_start(T.xs[:], T.x[:])], [], ["xs"])
    D("Y", 8300, lambda g, T, e: [g.sync.dma_start(T.cs[:], T.c0[:])], [], ["c%d" % s for s in range(NS)])
    D("Y", 8600, lambda g, T, e: [g.sync.dma_start(T.y0s[:], T.y0[:]), g.sync.dma_start(T.hs[:, 0:1], T.h[:])], [], ["y0s", "hs"], n=2)
    io("io1", 16, [[-1, 16]], 16, 1)
    io("ie", 144, [[-1, 144]], 15, 1)
    io("idn", 128, [[-1, 128]], 0, 1)
    io("ib", 128, [[-1, 16], [-16, 8]], 0, 1)
    io("im", 8, [[-16, 8]], 0, 1)
    io("ic", 128, [[-1, 16], [-32, 4], [1000, 2]], 0, 1)
    io("ia", 128, [[-1, 8], [-8, 16]], 0, 1)
    io("i16", 16, [[1, 16]], 0, 16)
    io("i512", 512, [[1, 512]], 0, 0)
    io("adjd", 2048, [[-1, 2048]], 0, 0)
    D("G", 5300, lambda g, T, e: [g.dma_start(T.adjd[:], T.adj[:], accum_op=A.add)], ["adjs"], ["adjd"])
    D("Y", 5300, lambda g, T, e: [g.sync.dma_start(T.adjp[16 * k + 1:16 * k + 16, :], T.adj[16 * k:16 * k + 15, :]) for k in range(8)]
      + [g.sync.dma_start(T.adjp[16 * k:16 * k + 1, :], T.i16[:]) for k in range(8)], ["i16", "xs"], ["adjp"], n=16)
    IDT = ["idt%d" % k for k in range(4)]
    for k in range(4): S(512, act(C("idt", 512 * k, 512 * k + 512), B("i512"), bias=float(512 * k)), ["i512"], [IDT[k]])
    V(16, ts(B("io2"), B("io1"), 15, None, A.bitwise_and), ["io1"], ["io2"])
    V(16, ms(C("oh", 16, 32), 0.0), [], ["oh1"])
    V(16, ts(C("oh", 0, 16), B("io2"), 0.0, None, EQ), ["io2"], ["oh0"])
    V(16, cp(C("imf", 0, 1), C("io2", 0, 1)), ["io2"], ["pmod"])
    V(144, ts(B("ez"), B("ie"), C("imf", 0, 1), None, EQ), ["ie", "pmod"], ["ez"])
    for a, b in (("idf", "idn"), ("pmt", "ib"), ("pm", "ia"), ("idh", "idn")):
        V(128, ts(B(a), B(b), 0.0, None, EQ), [b], [a])
    V(128, cp(B("pmth"), B("pmt")), ["pmt"], ["pmth"])
    V(128, ts(B("nidh"), B("idh"), -1.0, None, A.mult), ["idh"], ["nidh"], f=0.5)
    S(128, act(B("idb"), B("idf")), ["idf"], ["idb"])
    S(128, act(B("nidb"), B("idf"), scale=-1.0), ["idf"], ["nidb"])
    V(8, ts(B("im2"), B("im"), 4, None, A.arith_shift_right), ["im"], ["im2"])
    V(8, ts(B("m8"), B("im2"), 0.0, None, EQ), ["im2"], ["m8"])
    S(8, act(B("m8s"), B("m8"), scale=SC), ["m8"], ["m8s"])
    PT = ["pt%d" % k for k in range(4)]
    for k in range(4): V(128, ts(B("pt", al, k, al), B("ic"), float(16 * (k // 2)) + 1000.0 * (k % 2), None, EQ), ["ic"], [PT[k]])
    S(56, act(B("hz"), C("idn", 0, 56), scale=0.0), ["idn"], ["hz"])
    V(8, ts(C("hz", 24, 32), B("m8"), C("hs", 0, 1), None, A.mult), ["m8", "hs"], ["hz"])
    S(56, act(B("oz"), C("idn", 0, 56), scale=0.0), ["idn"], ["oz"])
    S(8, act(C("oz", 24, 32), B("m8"), scale=SC), ["m8"], ["oz"])
    S(8, act(C("imf", 1, 2), C("imf", 0, 1), bias=-16.0), ["pmod"], ["pm16"])
    V(8, ts(B("jm"), B("m8"), C("imf", 1, 2), None, A.mult), ["m8", "pm16"], ["jm"])
    V(136, ms(B("dn"), 4096.0), [], ["dn"])
    V(16, ms(C("dn", 0, 136, 17), -float(2 ** 31)), [], ["dn"])
    V(16, cp(B("j16"), B("j0s")), ["j0s"], ["j16"])
    V(16, cp(B("v0h"), B("v0s")), ["v0s"], ["v0h"])
    V(16, ts(B("b0h"), B("j0s"), 16.0, None, A.is_ge), ["j0s"], ["b0h"])
    V(16, tt(B("bv0"), B("b0h"), B("v0h"), A.mult), ["b0h", "v0h"], ["bv0"])

    def stream(s):
        L, l0 = LS[s], L0[s]
        R, k0 = L // 16, l0 // 16
        n = lambda x: "%s%d" % (x, s)
        N = lambda *x: [n(y) for y in x]
        bN, bK, bW, bE = range(4 * s, 4 * s + 4)
        pK, pN, pW, pE = ["ps%d" % b for b in (bK, bN, bW, bE)]
        kp = C(pK, 0, 17 * R); nb = B(pN, al, slice(0, R), slice(0, 17))
        nb0, d_ = B(pN, al, slice(0, R), 0), B(pN, al, slice(0, R), 17)
        VP, WP, VU, AG, ag_ = C(pW, 0, 2 * R), C(pW, 32, 32 + R), C(pE, 0, R), C(pE, 16, 16 + R), C(pE, 24, 24 + R)
        DP, CP = C(pE, 32, 32 + L), C(pE, 32 + L, 32 + 2 * L)
        JP = B(pK, slice(0, 8), slice(0, L))
        v_, b_, bq_, e_, eq_, t1_, t2_, t3_, an_ = [B(n("sm"), al, j, al) for j in range(9)]
        cS = C("cs", l0, l0 + L)
        v16, u16, w16 = C(n("vu"), 0, R), C(n("vu"), R, 2 * R), B(n("w16"))
        NP = (L + PIECE - 1) // PIECE
        pk = lambda x: [n(x) + "_%d" % j for j in range(NP)]
        CZ = [n("cz") + "_%d" % q for q in range(8)]

        def stations(more):
            for q in range(8):
                def put(g, T, e, q=q):
                    o = T[n("cz")][:, 24 + q:32 * L:32]
                    if e == "V": return g.vector.tensor_scalar(o, cS(T), T.m8s[:, q:q + 1], None, A.mult)
                    return g.scalar.activation(o, cS(T), F.Identity, scale=T.m8s[:, q:q + 1])
                i = op("F", (64.0, 0, 0, 128.0), put, [n("c"), "m8s"] + more, [CZ[q]])
                ops[i]["fix"] = "S" if q % 4 == 0 else "V"

        def to_u(T, ps, a, b, st, z, y):
            return sum([grp(T[ps][32 * q:32 * q + 32, a:b:st], [(T[z][:, 24 - 8 * c:56 - 8 * c], y(T)[:, 4 * q + c::16]) for c in range(4)]) for q in range(4)], [])

        def again(y, ykey):
            P(512, mms(lambda T: to_u(T, pE, 16, 16 + R, None, "hz", y)), [ykey, "hz"], N("AG"), [bE])
            V(R, cp(B(n("gi"), al, 0, al), AG), N("AG"), N("gi0"), [bE])
            V(R, ts(B(n("gi"), al, 1, al), B(n("gi"), al, 0, al), 2047, None, A.bitwise_and), N("gi0"), N("gi1"))
            V(R, cp(an_, B(n("gi"), al, 1, al)), N("gi1"), N("an"))

        def masks():
            X("S", L, act(B(n("ur")), ind("idt", u16)), IDT + N("vu"), N("ur"))
            X("V", L, tt(B(n("mk")), ind("adjp", v16), B(n("ur")), EQ), ["adjp"] + N("vu", "ur"), N("mk"))

        tag[0] = ("i", s); tag[1] = 0
        zs = []
        for a in range(0, 32 * L + 32, 1032):
            zs.append(n("z") + str(a)); b = min(a + 1032, 32 * L + 32)
            V(b - a, ms(C(n("cz"), a, b), 0.0), [], [zs[-1]], f=0.5)
        V(R, cp(v16, C("v0s", k0, k0 + R)), ["v0s"], N("vu"))
        stations(zs)
        P(64, mms(lambda T: grp(VU(T), [(T.pmth[:], T.v0h[:, k0:k0 + R])])), ["pmth", "v0h"], N("VU"), [bE])
        V(R, cp(v_, VU), N("VU"), N("v"), [bE])
        again(C("y0s", l0, l0 + L), "y0s")
        X("S", L, act(B(n("mk")), ind("oh", C("j16", k0, k0 + R))), ["oh0", "oh1", "j16"], N("mk"))
        yield

        for t in range(1, STEPS + 1):
            tag[0] = (s, t); tag[1] = 0
            tab = "adjs" if t == 1 else "adjd"
            if t > 1: masks()
            X("V", L, tt(B(n("pr")), ind(tab, v16), B(n("mk")), A.mult), [tab] + N("vu", "mk"), N("pr"))
            if t == 1: P(64, mms(lambda T: grp(WP(T), [(T.idh[:], T.bv0[:, k0:k0 + R])], True, False)), ["idh", "bv0"], N("WP"), [bW])
            P(1024, mms(lambda T: grp(WP(T), [(T.ez[:, 15 - j:143 - j], T[n("pr")][:, j::16]) for j in range(16)], False, True)), ["ez", n("pr")], N("WP"), [bW])
            V(R, cp(w16, WP), N("WP"), N("w16"), [bW])
            X("V", L, cp(B(n("nb16")), ind("adjs", w16)), ["adjs", n("w16")], N("nb16"))
            X("V", L, tt(B(n("xw")), ind("xs", w16), cS, A.mult), ["xs"] + N("w16", "c"), N("xw"))
            P(512, mms(lambda T: to_u(T, pK, 0, 17 * R, 17, "oz", B(n("xw")))), ["oz", n("xw")], N("K0"), [bK])
            S(R, act(B(n("wf")), WP), N("WP"), N("wf"), [bW])
            V(L, cp(B(n("nbf")), B(n("nb16"))), N("nb16"), N("nbf"), f=0.5)
            V(L, lambda g, T, e: g.vector.transpose(T[n("nbt")][:], T[n("nbf")][:]), N("nbf"), N("nbt"), f=0.5)
            P(832, mms(lambda T: grp(nb0(T), [(T.pmt[:], T[n("wf")][:])]) + grp(d_(T), [(T.pmt[:], T[n("wf")][:]), (T.nidh[:], v_(T))]) + sum(
                [grp(T[pN][:, c:R:2, 1:17], [(T.pt[:, 2 * c + z, :], T[n("nbt")][:, :, z, :]) for z in range(2)]) for c in range(2)], [])),
              ["pmt", "nidh"] + N("wf", "nbt", "v") + PT, N("NB"), [bN])
            V(R, ts(b_, d_, 0.0, None, EQ), N("NB"), N("b"), [bN])
            P(128, mms(lambda T: grp(ag_(T), [(T.idh[:], an_(T)), (T.nidh[:], v_(T))])), ["idh", "nidh"] + N("an", "v"), N("ag"), [bE])
            V(R, tt(bq_, b_, ag_, A.mult), N("b", "ag"), N("bq"), [bE])
            for j in range(NP):
                a, b = j * PIECE, min(L, (j + 1) * PIECE)
                def big(g, T, e, a=a, b=b):
                    o = T[n("xg")][:, 16 * a:16 * b]; i = T.xs[:].indirect(T[n("nb16")][:, a:b])
                    return g.vector.tensor_copy(o, i) if e == "V" else g.scalar.activation(o, i, F.Identity)
                i = X("F", 16 * (b - a), big, ["xs", n("nb16")], [pk("xg")[j]])
                ops[i]["fix"] = "V" if j >= NP - NV else "S"
                P(32 * (b - a), mms(lambda T, a=a, b=b: [
                    (T[pK][32 * (m % 16 // 4):32 * (m % 16 // 4) + 32, 17 * (m // 16) + 1:17 * (m // 16) + 17],
                     T[n("cz")][:, 32 * m + 24 - 8 * (m % 4):32 * m + 56 - 8 * (m % 4)],
                     T[n("xg")][:, 16 * m:16 * m + 16], m % 4 == 0, m % 4 == 3) for m in range(a, b)]),
                  CZ + [pk("xg")[j]], [pk("KP")[j]], [bK])
            s1, s2, s3 = B(n("s1")), B(n("s2")), B(n("s3"))
            V(17 * R, scan(s1, B("dn"), kp, A.add, A.max), pk("KP") + ["dn", n("K0")], N("s1"), [bK])
            V(17 * R, tt(s2, s1, kp, A.subtract), pk("KP") + N("s1", "K0"), N("s2"), [bK])
            V(17 * R, tt(s3, nb, s2, A.subtract), N("NB", "s2"), N("s3"), [bN])
            V(17 * R, scan(s1, s2, s3, A.min, A.max), N("s2", "s3"), N("s1"))
            p_ = C(n("s1"), 16, 17 * R, 17)
            V(R, tt(eq_, p_, v_, EQ), N("s1", "v"), N("eq"))
            V(R, tt(e_, p_, v_, A.subtract), N("s1", "v"), N("e"))
            V(R, tt(t2_, eq_, d_, A.mult), N("eq", "NB"), N("t2"), [bN])
            V(R, tt(t1_, e_, b_, A.mult), N("e", "b"), N("t1"))
            V(R, tt(t3_, eq_, bq_, A.mult), N("eq", "bq"), N("t3"))
            tv = lambda T, m: [(T[m][:], y(T)) for y in (v_, t2_, t1_, t3_)]
            TV = N("v", "t1", "t2", "t3")
            P(576, mms(lambda T: grp(T[pW][:, R:2 * R], [(T.idf[:], T[n("wf")][:]), (T.pm[:], t3_(T))]) + grp(T[pW][:, 0:R], tv(T, "pm"))),
              ["pm", "idf", n("wf")] + TV, N("VP"), [bW])
            V(2 * R, cp(B(n("vu")), VP), N("VP"), N("vu"), [bW])
            if t < STEPS:
                P(256, mms(lambda T: grp(VU(T), tv(T, "idh"))), ["idh"] + TV, N("VU"), [bE])
                P(256, mms(lambda T: grp(WP(T), tv(T, "pm"), True, False)), ["pm"] + TV, N("WP"), [bW])
                V(R, cp(v_, VU), N("VU"), N("v"), [bE])
            if t % 2 == 0:
                x = t // 2 - 1
                xv, ld, kx, kl = B(n("xv"), al, x, al), B(n("ld"), al, x, al), n("xv") + str(x), n("ld") + str(x)
                X("S", L, act(xv, ind("xs", v16)), ["xs", n("vu")], [kx])
                sd = op("G", (300.0, 0, 0, 0), (n("ld"), n("xv"), x, "a%d" % (4 * s + x)), [kx], [], kind="r")
                rv = op("R", (0, 0, 0, 0), None, [], [kl], lat=2000.0, kind="a")
                ops[rv]["deps"].add(sd); ops[rv]["sem"] = "a%d" % (4 * s + x)
                P(2 * L, mms(lambda T, xv=xv, ld=ld: grp(DP(T), [(T.nidb[:], xv(T)), (T.idb[:], ld(T))])), ["idb", "nidb", kx, kl], N("DP"), [bE])
                S(L, act(B(n("sg")), DP, F.Sign), N("DP"), N("sg"), [bE])
                P(2 * L, mms(lambda T: grp(CP(T), [(T.idb[:], cS(T)), (T.idb[:], T[n("sg")][:])])), ["idb"] + N("c", "sg"), N("CP"), [bE])
                if t < STEPS:
                    V(L, ts(cS, CP, 15.0, -15.0, A.min, A.max), N("CP"), N("c"), [bE])
                    stations([])
                    again(ld, kl)
                else:
                    co, vr = C("cof", l0, l0 + L), C("vr", l0, l0 + L)
                    V(L, ts(co, CP, 15.0, -15.0, A.min, A.max), N("CP"), N("co"), [bE])
                    D("Y", 300, lambda g, T, e: [g.sync.dma_start(T.co[:, l0:l0 + L], co(T))], N("co"), [])
                    masks()
                    P(L, mms(lambda T: grp(JP(T), [(T.jm[:], T[n("mk")][:])])), ["jm", n("mk")], N("JP", "K0") + pk("KP"), [bK])
                    S(L, act(lambda T: T.jr[0:8, l0:l0 + L], JP, bias=16.0), N("JP"), N("jr"), [bK])
                    D("Y", 100, lambda g, T, e: [g.sync.dma_start(T.jo[:, l0:l0 + L], T.jr[0:8, l0:l0 + L])], N("jr"), [])
                    X("S", L, act(vr, ind("idt", v16)), IDT + N("vu"), N("vr"))
                    D("Y", 100, lambda g, T, e: [g.sync.dma_start(T.vo[:, l0:l0 + L], T.vr[0:128:16, l0:l0 + L])], N("vr"), [])
            yield

    gens = [stream(s) for s in range(NS)]
    for t in range(STEPS + 1):
        for x in gens: next(x)
    return ops


def cost(o, e, m):
    c = o["cost"]
    return c[0] + m[0] * c[1] + m[2] * c[2] + (c[3] if e == "S" else 0.0) + (m[3] if e in "VS" else 0.0)


def place(ops, order, on, m):
    free = dict.fromkeys("VSPGYR", 0.0); fin = [0.0] * len(ops)
    for i in order:
        o = ops[i]; e = on[i]; t = free[e]
        for d in o["deps"]:
            if fin[d] > t: t = fin[d]
        t += cost(o, e, m); free[e] = t
        fin[i] = t + o["lat"] + m[1]
    return max(fin)


def fit(key, pred, succ, cs, lat, on, back):
    n = len(key)
    if back: pred, succ = succ, pred
    left = [len(p) for p in pred]; rd = [i for i in range(n) if not left[i]]
    busy = {e: ([], []) for e in "VSPGYR"}; st = [0.0] * n; fi = [0.0] * n
    while rd:
        i = min(rd, key=lambda j: key[j])
        rd.remove(i)
        t = 0.0
        for j in pred[i]:
            z = fi[j] + (lat[i] if back else lat[j])
            if z > t: t = z
        if back and not pred[i]: t = lat[i]
        c = cs[i][on[i]]; a, b = busy[on[i]]; k = len(b)
        while k and b[k - 1] > t: k -= 1
        while k < len(a) and a[k] < t + c:
            t = max(t, b[k]); k += 1
        a.insert(k, t); b.insert(k, t + c); st[i] = t; fi[i] = t + c
        for j in succ[i]:
            left[j] -= 1
            if not left[j]: rd.append(j)
    return st, fi


def search(ops):
    n = len(ops); m = MODELS[0]
    pred = [sorted(o["deps"]) for o in ops]
    succ = [[] for _ in ops]
    for i in range(n):
        for d in pred[i]: succ[d].append(i)
    cs = [{e: cost(o, e, m) for e in ("SV" if o["eng"] == "F" else o["eng"])} for o in ops]
    lat = [o["lat"] + m[1] for o in ops]
    on = [o.get("fix", o["eng"]) for o in ops]
    flex = [i for i in range(n) if ops[i]["eng"] == "F"]
    base = [0.0] * n
    for i in range(n - 1, -1, -1): base[i] = cs[i][on[i]] + lat[i] + max([base[j] for j in succ[i]] + [0.0])
    seed = [12345]
    def rnd():
        seed[0] = (seed[0] * 6364136223846793005 + 1442695040888963407) % (1 << 64)
        return (seed[0] >> 33) / float(1 << 31)
    def sid(o): return o["tag"][0][0] if isinstance(o["tag"][0][0], int) else 0
    key = [-base[i] + 9000.0 / NS * sid(ops[i]) for i in range(n)]
    best = cur = None
    for it in range(ITER):
        for r in range(2):
            for i in range(5): key[i] = -1e9 + i
            st, fi = fit(key, pred, succ, cs, lat, on, False)
            order = sorted(range(n), key=lambda i: (st[i], i))
            sc = sum(place(ops, order, on, q) for q in MODELS) / len(MODELS)
            if cur is None or sc < cur[0] + 120.0 * (1.0 - it / float(ITER)): cur = (sc, order, list(on), st)
            if best is None or sc < best[0]: best = (sc, order, list(on), st)
            key = [-x for x in fit([-(fi[i] + lat[i]) for i in range(n)], pred, succ, cs, lat, on, True)[1]]
        c = rnd() * cur[0]; w = (2000.0, 6000.0, 1e5)[int(rnd() * 3)]; a = (200.0, 800.0, 2000.0)[int(rnd() * 3)]
        key = [x + ((rnd() - 0.5) * a if abs(x - c) < w else 0.0) for x in cur[3]]
        on = list(cur[2])
        if rnd() < 0.5:
            i = flex[int(rnd() * len(flex))]; on[i] = "V" if on[i] == "S" else "S"
    return best


PLAN = {}


def plan():
    if not PLAN:
        ops = build()
        sc, order, on, st = search(ops)
        cnt = dict.fromkeys("VSPG", 0)
        known = {e: {} for e in "VSPGY"}
        total = {}
        for i in order:
            o = ops[i]; e = o["on"] = on[i]; o["st"] = st[i]
            if o["kind"] == "a":
                o["sig"] = (o["sem"], NENG); o["clock"] = {o["sem"]: NENG}; total[o["sem"]] = NENG
                continue
            waits = []
            kn = known[e]
            for d in sorted(o["deps"], key=lambda j: -ops[j]["st"]):
                sem, c = ops[d]["sig"]
                if (e == "P" and sem == "P") or kn.get(sem, 0) >= c: continue
                waits.append((sem, c))
                for k, v in ops[d]["clock"].items():
                    if kn.get(k, 0) < v: kn[k] = v
            o["waits"] = waits
            if o["kind"] == "d": o["sig"] = (o["sem"], 16 * o["n"])
            elif o["kind"] == "r": o["sig"] = ("loc", total.get("loc", 0) + NENG)
            else:
                cnt[e] += 1; o["sig"] = (e, cnt[e])
            total[o["sig"][0]] = o["sig"][1]
            o["clock"] = dict(kn); o["clock"][o["sig"][0]] = o["sig"][1]
        PLAN["ops"] = ops; PLAN["order"] = order; PLAN["total"] = total; PLAN["on"] = on
    return PLAN


def rank_program(g, core, T, topo):
    rank = T.rank_of(core)
    if rank is None:
        return
    pl = plan()
    nxt = T.cores[(rank + 1) % len(T.cores)]
    rid, pid = topo.addr(nxt)[:2]
    mask = sum(1 << e for e in topo.engines(core, nxt)[:NENG])
    q = {"V": g.vector, "S": g.scalar, "P": g.tensor, "G": g, "Y": g.sync}
    for i in pl["order"]:
        o = pl["ops"][i]
        if o["kind"] == "a": continue
        e = o["on"]
        for sem, c in o["waits"]: q[e].wait_ge(T.sem[sem], c)
        if o["kind"] == "r":
            ld, xv, x, sem = o["fn"]
            g.remote_dma(T[ld][:, x, :], T[xv][:, x, :], T.sem[sem], T.sem["loc"], pid, rid, mask)
        elif o["kind"] == "d":
            for ins in o["fn"](g, T, e): ins.then_inc(T.sem[o["sem"]], 16)
        else:
            o["fn"](g, T, e).then_inc(T.sem[e], 1)
    for sem, c in pl["total"].items():
        g.wait_ge(T.sem[sem], c)
